import numpy as np
import ml_dtypes


def mxq(x, axis, fmt="e4m3"):
    dtype, down = {"e4m3": (ml_dtypes.float8_e4m3fn, 7), "e5m2": (ml_dtypes.float8_e5m2, 14)}[fmt]
    v = np.moveaxis(np.asarray(x, np.float32).astype(ml_dtypes.bfloat16).astype(np.float64), axis, -1)
    blocks = v.reshape(v.shape[:-1] + (-1, 32))
    amax = np.abs(blocks).max(-1, keepdims=True)
    byte = np.maximum(np.where(amax > 0, np.frexp(amax)[1] - 1 + 127, 0) - down, 1)
    scale = np.exp2(byte - 127.0)
    codes = (blocks / scale).astype(np.float32).astype(dtype).astype(np.float64)
    return np.moveaxis((codes * scale).reshape(v.shape), -1, axis)


WIDE = False


def mx_kscale(k):
    if not WIDE:
        return np.ones(k)
    levels = np.array([10, -10, 5, -5, 0])
    if k % 512:
        return np.exp2(np.random.permutation(np.resize(levels, k // 32))).repeat(32)
    a = np.empty((k // 512, 16))
    for p in range(k // 512):
        a[p, :8] = np.random.permutation(np.resize(levels, 8))
        for g in range(8):
            far = levels[np.abs(levels - a[p, g]) >= 10]
            a[p, g + 8] = far[np.random.randint(len(far))]
    return np.exp2(a.ravel()).repeat(32)


def f64(x):
    return np.asarray(x).astype(np.float64)


def striped(idx):
    return np.tile(idx.reshape(-1, 16).T, (8, 1)).astype(np.uint16)


def unstriped(offs):
    return offs[:16].T.reshape(-1).astype(np.int64)


def striped8(idx):
    return np.concatenate([x.reshape(-1, 16).T for x in idx]).astype(np.uint16)


def runs(offs, k):
    lists = np.stack([offs[16 * r : 16 * r + 16].T.reshape(-1) for r in range(8)]).astype(np.int64)
    return lists[np.arange(k) % 512 // 64]


def pack_weight(w):
    k, n = w.shape
    w = f64(np.asarray(w, np.float32).astype(ml_dtypes.bfloat16)).reshape(k // 32, 32, n)
    amax = np.abs(w).max(1)
    byte = np.clip(np.where(amax > 0, np.frexp(amax)[1] - 1 + 127 - 7, 1), 1, 254)
    scaled = (w * np.exp2(127.0 - byte)[:, None, :]).reshape(k, n).astype(np.float32)
    words = np.ascontiguousarray(scaled.reshape(k // 512, 128, 4, n).transpose(0, 1, 3, 2)).astype(ml_dtypes.float8_e4m3fn).view(np.uint8)
    return words, np.ascontiguousarray(byte.astype(np.uint8).reshape(k // 512, 16, n))


def unpack_weight(words, scales):
    g, p, n, _ = words.shape
    vals = np.ascontiguousarray(words).view(ml_dtypes.float8_e4m3fn).astype(np.float64) * np.repeat(np.exp2(scales.astype(np.float64) - 127.0), 8, axis=1)[..., None]
    return vals.transpose(0, 1, 3, 2).reshape(g * 512, n)


E2M1 = np.array([0.0, 0.5, 1.0, 1.5, 2.0, 3.0, 4.0, 6.0, -0.0, -0.5, -1.0, -1.5, -2.0, -3.0, -4.0, -6.0])


def pack_fp4(w):
    k, n = w.shape
    w = f64(np.asarray(w, np.float32).astype(ml_dtypes.bfloat16)).reshape(k // 32, 32, n)
    amax = np.abs(w).max(1)
    mant, ex = np.frexp(amax / 6.0)
    byte = np.clip(np.where(amax > 0, np.where(mant > 0.5, ex, ex - 1) + 127, 1), 1, 254)
    scaled = (w * np.exp2(127.0 - byte)[:, None, :]).reshape(k, n).astype(np.float32)
    c = np.ascontiguousarray(scaled.reshape(k // 512, 128, 4, n).transpose(0, 1, 3, 2)).astype(ml_dtypes.float4_e2m1fn).view(np.uint8) & 0xF
    words = (c[..., 0::2] | (c[..., 1::2] << 4)).reshape(k // 512, 128, 2 * n)
    return np.ascontiguousarray(words), np.ascontiguousarray(byte.astype(np.uint8).reshape(k // 512, 16, n))


def unpack_fp4(words, scales):
    g, _, n = scales.shape
    words = np.ascontiguousarray(words).reshape(g, 128, n, 2)
    nib = np.empty((g, 128, n, 4), np.uint8)
    nib[..., 0::2] = words & 0xF
    nib[..., 1::2] = words >> 4
    vals = E2M1[nib] * np.repeat(np.exp2(scales.astype(np.float64) - 127.0), 8, axis=1)[..., None]
    return vals.transpose(0, 1, 3, 2).reshape(g * 512, n)


def planes(y):
    n, m = y.shape
    v = y.astype(np.float32).astype(ml_dtypes.bfloat16).astype(np.float64).reshape(n // 32, 32, m)
    top = np.abs(v).max(1)
    byte = np.clip(np.where(top > 0, np.frexp(top)[1] - 1 + 127 - 7, 1), 1, 254)
    codes = (v * np.exp2(127.0 - byte)[:, None, :]).reshape(n, m).astype(np.float32).astype(ml_dtypes.float8_e4m3fn).view(np.uint8)
    words = codes.reshape(n // 512, 128, 4, m).transpose(0, 1, 3, 2)
    return np.ascontiguousarray(words), np.ascontiguousarray(byte.astype(np.uint8).reshape(n // 512, 16, m))


K, T, S, N, H = 512, 2048, 512, 512, 512


def setup_inputs():
    n = np.random.standard_normal
    s = mx_kscale(K)[:, None]
    u = mx_kscale(H)
    packed_xT = pack_weight(n((K, T)) * s)
    packed_w1 = pack_fp4(n((K, H)) / np.sqrt(K) / s)
    packed_w2 = pack_fp4(n((H, N)) / np.sqrt(H) / u[:, None])
    packed_w3 = pack_fp4(n((K, N)) / np.sqrt(K) / s)
    return {
        "x_words": packed_xT[0],
        "x_scales": packed_xT[1],
        "w1_words": packed_w1[0],
        "w1_scales": packed_w1[1],
        "gn": (np.random.uniform(0.5, 1.5, (H, 1)) * u[:, None]).astype(np.float32),
        "w2_words": packed_w2[0],
        "w2_scales": packed_w2[1],
        "w3_words": packed_w3[0],
        "w3_scales": packed_w3[1],
        "offs": striped(np.random.permutation(T)[:S]),
        "n1": striped8(np.stack([np.random.permutation(S) for _ in range(8)])),
        "n2": striped8(np.stack([np.random.permutation(S) for _ in range(8)])),
        "two": striped(np.random.permutation(T)[:S]),
        "n3": striped8(np.stack([np.random.permutation(S) for _ in range(8)])),
        "n4": striped8(np.stack([np.random.permutation(S) for _ in range(8)])),
        "n5": striped8(np.stack([np.random.permutation(S) for _ in range(8)])),
    }


def reference(x_words, x_scales, w1_words, w1_scales, gn, w2_words, w2_scales, w3_words, w3_scales, offs, n1, n2, two, n3, n4, n5):
    x_two = unpack_weight(x_words, x_scales)[:, unstriped(two)]
    d = unpack_fp4(w3_words, w3_scales).T @ x_two
    xq = unpack_weight(x_words, x_scales)[:, unstriped(offs)]
    y = unpack_fp4(w1_words, w1_scales).T @ xq
    sq = (y) ** 2
    z = f64(gn) * ((y[np.arange(H)[:, None], runs(n2, H)]) / (np.sqrt(sq + sq[np.arange(H)[:, None], runs(n1, H)] + 0.25)))
    h = unpack_fp4(w2_words, w2_scales).T @ mxq(z, 0, "e4m3")
    out_0 = d * (h[np.arange(N)[:, None], runs(n3, N)] - h) + 0.5 * ((d[np.arange(N)[:, None], runs(n5, N)]) * (h[np.arange(N)[:, None], runs(n4, N)] - h))
    return (out_0,) + planes(out_0)

@@ -1,0 +1,195 @@
+from contextlib import ExitStack
+
+import concourse.mybir as mybir
+
+K, T, S, N, H = 512, 2048, 512, 512, 512
+FLOPS = 3 * 2 * 512 * 512 * 512
+
+F32 = mybir.dt.float32
+BF16 = mybir.dt.bfloat16
+I32 = mybir.dt.int32
+U32 = mybir.dt.uint32
+U16 = mybir.dt.uint16
+U8 = mybir.dt.uint8
+FP8X4 = mybir.dt.float8_e4m3fn_x4
+FP4X4 = mybir.dt.float4_e2m1fn_x4
+ACT = mybir.ActivationFunctionType
+ALU = mybir.AluOpType
+
+P = 128
+PACK = 4
+LIST_ROWS = 16
+CHUNKS = ((0, 256), (256, 384), (384, 512))
+
+
+def tile_picked_lateflowbrms_none_po_kernel(
+    tc, x_words, x_scales, w1_words, w1_scales, gn, w2_words, w2_scales, w3_words, w3_scales,
+    offs, n1, n2, two, n3, n4, n5, out_0, out_1, out_2,
+):
+    nc = tc.nc
+    with ExitStack() as ctx:
+        held = ctx.enter_context(tc.tile_pool(name="held", bufs=1))
+        psum = ctx.enter_context(tc.psum_pool(name="psum", bufs=1))
+
+        def load_list(src, name):
+            lst = held.tile([P, S // LIST_ROWS], U16, name=name)
+            nc.sync.dma_start(lst[:], src)
+            return lst
+
+        def load_scale_rows(queues, clear, src, width, name):
+            plane = held.tile([P, width], U8, name=name, align_bytes=64)
+            clear.memset(plane[:].bitcast(I32), 0)
+            for q, queue in enumerate(queues):
+                queue.dma_start(plane[32 * q : 32 * q + 4, :].bitcast(I32), src[0, 4 * q : 4 * q + 4, :].bitcast(I32))
+            return plane
+
+        def load_weight_words(queue, src, name):
+            raw = held.tile([P, 2 * H], U8, name=name, align_bytes=64)
+            queue.dma_start(raw[:].bitcast(I32), src[0].bitcast(I32))
+            return raw
+
+        def deal_words(raw, name):
+            words = held.tile([P, 2 * H], U8, name=name, align_bytes=64)
+            nc.vector.tensor_copy(
+                words[:].rearrange("p (t m b) -> p t m b", t=PACK, b=2),
+                raw[:].rearrange("p (m t b) -> p t m b", t=PACK, b=2),
+            )
+            return words
+
+        def deal_scales(plane, name):
+            scales = held.tile([P, H], U8, name=name, align_bytes=64)
+            nc.vector.tensor_copy(
+                scales[:].rearrange("p (t m) -> p t m", t=PACK),
+                plane[:].rearrange("p (m t) -> p t m", t=PACK),
+            )
+            return scales
+
+        def pick(lst, name, words_tag, scales_tag):
+            words = held.tile([P, S], U32, name=name + "_words", tag=words_tag, align_bytes=64)
+            scales = held.tile([P, S], U8, name=name + "_scales", tag=scales_tag, align_bytes=64)
+            nc.vector.tensor_copy(words[:], xw[:].bitcast(U32).indirect(lst[:]))
+            nc.vector.tensor_copy(scales[:], xs[:].indirect(lst[:]))
+            return words, scales
+
+        def product(acc, weight, t, words, scales):
+            nc.tensor.matmul_mx(
+                out=acc,
+                lhsT=weight[0][:, 2 * P * t : 2 * P * (t + 1)].bitcast(FP4X4),
+                lhsT_scale=weight[1][:, P * t : P * (t + 1)],
+                rhs=words.bitcast(FP8X4),
+                rhs_scale=scales,
+                start=True,
+                stop=True,
+            )
+
+        def interleave(dst, src):
+            nc.scalar.copy(
+                dst[:].rearrange("p (c i t) -> p c t i", i=4, t=PACK),
+                src[:].rearrange("p t (c i) -> p c t i", i=4),
+            )
+
+        def entries(lst, lo, hi):
+            return lst[:, lo // LIST_ROWS : hi // LIST_ROWS]
+
+        l_offs = load_list(offs, "l_offs")
+        xw = held.tile([P, T], I32, name="xw")
+        nc.sync.dma_start(xw[:], x_words[0].rearrange("p n t -> p (n t)").bitcast(I32))
+        w1_raw = load_weight_words(nc.scalar, w1_words, "w1_raw")
+        w3_raw = load_weight_words(nc.scalar, w3_words, "w3_raw")
+        xs = load_scale_rows([nc.scalar] * 4, nc.vector, x_scales, T, "xs")
+        w1_plane = load_scale_rows([nc.sync, nc.sync, nc.gpsimd, nc.gpsimd], nc.gpsimd, w1_scales, H, "w1_plane")
+        l_n1 = load_list(n1, "l_n1")
+        w2_raw = load_weight_words(nc.sync, w2_words, "w2_raw")
+        w2_plane = load_scale_rows([nc.sync] * 4, nc.vector, w2_scales, N, "w2_plane")
+        gain = held.tile([P, PACK], F32, name="gain")
+        nc.sync.dma_start(gain[:], gn.rearrange("(p t) o -> p (t o)", t=PACK))
+        l_n2 = load_list(n2, "l_n2")
+        w3_plane = load_scale_rows([nc.sync] * 4, nc.vector, w3_scales, N, "w3_plane")
+        l_two = load_list(two, "l_two")
+        l_n3 = load_list(n3, "l_n3")
+        l_n4 = load_list(n4, "l_n4")
+        l_n5 = load_list(n5, "l_n5")
+
+        quarter = held.tile([P, 1], F32, name="quarter")
+        nc.vector.memset(quarter[:], 0.25)
+        wide = [held.tile([P, 2 * S], F32, name="wide%d" % t) for t in range(PACK)]
+        for t in range(PACK):
+            nc.vector.memset(wide[t][:, S:], 0.0)
+
+        w1 = (deal_words(w1_raw, "w1_dealt"), deal_scales(w1_plane, "w1_dealt_scales"))
+        w3_dealt = deal_words(w3_raw, "w3_dealt")
+        xq_words, xq_scales = pick(l_offs, "xq", "xq_words", "xq_scales")
+        y_acc = [psum.tile([P, S], F32, name="y_acc%d" % t, tag="bank%d" % t) for t in range(PACK)]
+        for t in range(PACK):
+            product(y_acc[t][:], w1, t, xq_words[:], xq_scales[:])
+        w2 = (deal_words(w2_raw, "w2_dealt"), deal_scales(w2_plane, "w2_dealt_scales"))
+        w3 = (w3_dealt, deal_scales(w3_plane, "w3_dealt_scales"))
+
+        sq = [held.tile([P, S], F32, name="sq%d" % t) for t in range(PACK)]
+        den = [held.tile([P, S], F32, name="den%d" % t) for t in range(PACK)]
+        inv = [held.tile([P, S], F32, name="inv%d" % t, align_bytes=64) for t in range(PACK)]
+        yg = [held.tile([P, S], F32, name="yg%d" % t, align_bytes=64) for t in range(PACK)]
+        for t in range(PACK):
+            nc.scalar.activation(wide[t][:, :S], y_acc[t][:], ACT.Square)
+            nc.scalar.activation(sq[t][:], y_acc[t][:], ACT.Square)
+            nc.vector.tensor_tensor(den[t][:], wide[t][:].indirect(l_n1[:]), sq[t][:], ALU.add)
+        for t in range(PACK):
+            nc.scalar.activation(yg[t][:], y_acc[t][:], ACT.Copy, scale=gain[:, t : t + 1])
+            nc.scalar.activation(inv[t][:], den[t][:], ACT.Abs_reciprocal_sqrt, bias=quarter[:])
+
+        h_acc = [psum.tile([P, S], F32, name="h_acc%d" % t, tag="bank%d" % t) for t in range(PACK)]
+        h = [held.tile([P, S], F32, name="h%d" % t) for t in range(PACK)]
+        z_bf = []
+        for lo, hi in CHUNKS:
+            z = held.tile([P, PACK, hi - lo], F32, name="z%d" % lo)
+            for t in range(PACK):
+                nc.vector.tensor_tensor(z[:, t, :], yg[t][:].indirect(entries(l_n2, lo, hi)), inv[t][:, lo:hi], ALU.mult)
+            rounded = held.tile([P, PACK * (hi - lo)], BF16, name="z_bf%d" % lo, align_bytes=64)
+            interleave(rounded, z)
+            z_bf.append(rounded)
+        for (lo, hi), rounded in zip(CHUNKS, z_bf):
+            z_words = held.tile([P, hi - lo], U32, name="z_words%d" % lo, align_bytes=64)
+            z_scales = held.tile([P, hi - lo], U8, name="z_scales%d" % lo, align_bytes=64)
+            nc.vector.quantize_mx(out=z_words[:].bitcast(FP8X4), scales=z_scales[:], in_=rounded[:])
+            for t in range(PACK):
+                product(h_acc[t][:, lo:hi], w2, t, z_words[:], z_scales[:])
+
+        x2_words, x2_scales = pick(l_two, "x2", "yg3", "inv3")
+        d_acc = [psum.tile([P, S], F32, name="d_acc%d" % t, tag="bank%d" % (PACK + t)) for t in range(PACK)]
+        for t in range(PACK):
+            product(d_acc[t][:], w3, t, x2_words[:], x2_scales[:])
+
+        near = held.tile([P, PACK, S], F32, name="near")
+        far = [held.tile([P, S], F32, name="far%d" % t) for t in range(PACK)]
+        half_d = [held.tile([P, S], F32, name="half_d%d" % t) for t in range(PACK)]
+        for t in range(PACK):
+            nc.scalar.copy(wide[t][:, :S], h_acc[t][:])
+            nc.scalar.copy(h[t][:], h_acc[t][:])
+            diff = held.tile([P, S], F32, name="diff%d" % t)
+            nc.vector.tensor_tensor(diff[:], wide[t][:].indirect(l_n3[:]), h[t][:], ALU.subtract)
+            nc.vector.tensor_tensor(far[t][:], wide[t][:].indirect(l_n4[:]), h[t][:], ALU.subtract)
+            nc.vector.tensor_tensor(near[:, t, :], diff[:], d_acc[t][:], ALU.mult)
+        for t in range(PACK):
+            nc.scalar.activation(half_d[t][:], d_acc[t][:], ACT.Copy, scale=0.5)
+
+        out_rows = out_0.rearrange("(p t) j -> p t j", t=PACK)
+        out_words = out_1[0].rearrange("p n t -> p (n t)").bitcast(I32)
+        o_scales = held.tile([P, S], U8, name="o_scales", align_bytes=64)
+        o_bf = []
+        for lo, hi in CHUNKS:
+            term = held.tile([P, PACK, hi - lo], F32, name="term%d" % lo)
+            for t in range(PACK):
+                nc.vector.tensor_tensor(term[:, t, :], half_d[t][:].indirect(entries(l_n5, lo, hi)), far[t][:, lo:hi], ALU.mult)
+            res = held.tile([P, PACK, hi - lo], F32, name="res%d" % lo)
+            nc.vector.tensor_tensor(res[:], term[:], near[:, :, lo:hi], ALU.add)
+            nc.sync.dma_start(out_rows[:, :, lo:hi], res[:])
+            rounded = held.tile([P, PACK * (hi - lo)], BF16, name="o_bf%d" % lo, align_bytes=64)
+            interleave(rounded, res)
+            o_bf.append(rounded)
+        for (lo, hi), rounded in zip(CHUNKS, o_bf):
+            o_words = held.tile([P, hi - lo], U32, name="o_words%d" % lo, align_bytes=64)
+            nc.vector.quantize_mx(out=o_words[:].bitcast(FP8X4), scales=o_scales[:, lo:hi], in_=rounded[:])
+            nc.sync.dma_start(out_words[:, lo:hi], o_words[:].bitcast(I32))
+        for q in range(4):
+            queue = nc.sync if q % 2 else nc.scalar
+            queue.dma_start(out_2[0, 4 * q : 4 * q + 4, :].bitcast(I32), o_scales[32 * q : 32 * q + 4, :].bitcast(I32))

@@ -1,6 +1,7 @@
 from contextlib import ExitStack
 
 import concourse.mybir as mybir
+from concourse.masks import make_identity
 
 K, T, S, N, H = 512, 2048, 512, 512, 512
 FLOPS = 3 * 2 * 512 * 512 * 512
@@ -19,7 +20,8 @@ ALU = mybir.AluOpType
 P = 128
 PACK = 4
 LIST_ROWS = 16
-CHUNKS = ((0, 256), (256, 384), (384, 512))
+Z_CHUNKS = ((0, 128), (128, 384), (384, 512))
+OUT_CHUNKS = ((0, 256), (256, 384), (384, 512))
 
 
 def tile_picked_lateflowbrms_none_po_kernel(
@@ -48,28 +50,31 @@ def tile_picked_lateflowbrms_none_po_kernel(
             queue.dma_start(raw[:].bitcast(I32), src[0].bitcast(I32))
             return raw
 
-        def deal_words(raw, name):
-            words = held.tile([P, 2 * H], U8, name=name, align_bytes=64)
-            nc.vector.tensor_copy(
+        def deal_words(engine, raw, name, tag):
+            words = held.tile([P, 2 * H], U8, name=name, tag=tag, align_bytes=64)
+            engine.tensor_copy(
                 words[:].rearrange("p (t m b) -> p t m b", t=PACK, b=2),
                 raw[:].rearrange("p (m t b) -> p t m b", t=PACK, b=2),
             )
             return words
 
-        def deal_scales(plane, name):
-            scales = held.tile([P, H], U8, name=name, align_bytes=64)
-            nc.vector.tensor_copy(
+        def deal_scales(engine, plane, name, tag):
+            scales = held.tile([P, H], U8, name=name, tag=tag, align_bytes=64)
+            engine.tensor_copy(
                 scales[:].rearrange("p (t m) -> p t m", t=PACK),
                 plane[:].rearrange("p (m t) -> p t m", t=PACK),
             )
             return scales
 
-        def pick(lst, name, words_tag, scales_tag):
-            words = held.tile([P, S], U32, name=name + "_words", tag=words_tag, align_bytes=64)
-            scales = held.tile([P, S], U8, name=name + "_scales", tag=scales_tag, align_bytes=64)
+        def pick_words(lst, name, tag):
+            words = held.tile([P, S], U32, name=name, tag=tag, align_bytes=64)
             nc.vector.tensor_copy(words[:], xw[:].bitcast(U32).indirect(lst[:]))
+            return words
+
+        def pick_scales(lst, name, tag):
+            scales = held.tile([P, S], U8, name=name, tag=tag, align_bytes=64)
             nc.vector.tensor_copy(scales[:], xs[:].indirect(lst[:]))
-            return words, scales
+            return scales
 
         def product(acc, weight, t, words, scales):
             nc.tensor.matmul_mx(
@@ -82,30 +87,30 @@ def tile_picked_lateflowbrms_none_po_kernel(
                 stop=True,
             )
 
-        def interleave(dst, src):
-            nc.scalar.copy(
+        def interleave(copy, dst, src):
+            copy(
                 dst[:].rearrange("p (c i t) -> p c t i", i=4, t=PACK),
-                src[:].rearrange("p t (c i) -> p c t i", i=4),
+                src.rearrange("p t (c i) -> p c t i", i=4),
             )
 
         def entries(lst, lo, hi):
             return lst[:, lo // LIST_ROWS : hi // LIST_ROWS]
 
         l_offs = load_list(offs, "l_offs")
+        l_two = load_list(two, "l_two")
         xw = held.tile([P, T], I32, name="xw")
         nc.sync.dma_start(xw[:], x_words[0].rearrange("p n t -> p (n t)").bitcast(I32))
         w1_raw = load_weight_words(nc.scalar, w1_words, "w1_raw")
-        w3_raw = load_weight_words(nc.scalar, w3_words, "w3_raw")
-        xs = load_scale_rows([nc.scalar] * 4, nc.vector, x_scales, T, "xs")
-        w1_plane = load_scale_rows([nc.sync, nc.sync, nc.gpsimd, nc.gpsimd], nc.gpsimd, w1_scales, H, "w1_plane")
-        l_n1 = load_list(n1, "l_n1")
+        xs = load_scale_rows([nc.scalar] * 4, nc.gpsimd, x_scales, T, "xs")
+        w1_plane = load_scale_rows([nc.sync, nc.sync, nc.sync, nc.gpsimd], nc.gpsimd, w1_scales, H, "w1_plane")
         w2_raw = load_weight_words(nc.sync, w2_words, "w2_raw")
-        w2_plane = load_scale_rows([nc.sync] * 4, nc.vector, w2_scales, N, "w2_plane")
+        w3_raw = load_weight_words(nc.sync, w3_words, "w3_raw")
+        l_n1 = load_list(n1, "l_n1")
         gain = held.tile([P, PACK], F32, name="gain")
         nc.sync.dma_start(gain[:], gn.rearrange("(p t) o -> p (t o)", t=PACK))
         l_n2 = load_list(n2, "l_n2")
+        w2_plane = load_scale_rows([nc.sync] * 4, nc.vector, w2_scales, N, "w2_plane")
         w3_plane = load_scale_rows([nc.sync] * 4, nc.vector, w3_scales, N, "w3_plane")
-        l_two = load_list(two, "l_two")
         l_n3 = load_list(n3, "l_n3")
         l_n4 = load_list(n4, "l_n4")
         l_n5 = load_list(n5, "l_n5")
@@ -114,82 +119,123 @@ def tile_picked_lateflowbrms_none_po_kernel(
         nc.vector.memset(quarter[:], 0.25)
         wide = [held.tile([P, 2 * S], F32, name="wide%d" % t) for t in range(PACK)]
         for t in range(PACK):
-            nc.vector.memset(wide[t][:, S:], 0.0)
+            nc.scalar.activation(wide[t][:, S:], quarter[:].to_broadcast([P, S]), ACT.Abs_reciprocal_sqrt)
 
-        w1 = (deal_words(w1_raw, "w1_dealt"), deal_scales(w1_plane, "w1_dealt_scales"))
-        w3_dealt = deal_words(w3_raw, "w3_dealt")
-        xq_words, xq_scales = pick(l_offs, "xq", "xq_words", "xq_scales")
+        w1_dealt = deal_words(nc.vector, w1_raw, "w1_dealt", "w1_dealt")
+        xq_scales = pick_scales(l_offs, "xq_scales", "xq_scales")
+        xq_words = pick_words(l_offs, "xq_words", "xq_words")
+        w1 = (w1_dealt, deal_scales(nc.vector, w1_plane, "w1_dealt_scales", "w1_dealt_scales"))
         y_acc = [psum.tile([P, S], F32, name="y_acc%d" % t, tag="bank%d" % t) for t in range(PACK)]
         for t in range(PACK):
             product(y_acc[t][:], w1, t, xq_words[:], xq_scales[:])
-        w2 = (deal_words(w2_raw, "w2_dealt"), deal_scales(w2_plane, "w2_dealt_scales"))
-        w3 = (w3_dealt, deal_scales(w3_plane, "w3_dealt_scales"))
+        x2_scales = pick_scales(l_two, "x2_scales", "x2_scales")
+        w2_dealt = deal_words(nc.vector, w2_raw, "w2_dealt", "w2_dealt")
+        ident = held.tile([P, P], F32, name="ident")
+        make_identity(nc, ident[:])
 
-        sq = [held.tile([P, S], F32, name="sq%d" % t) for t in range(PACK)]
-        den = [held.tile([P, S], F32, name="den%d" % t) for t in range(PACK)]
-        inv = [held.tile([P, S], F32, name="inv%d" % t, align_bytes=64) for t in range(PACK)]
-        yg = [held.tile([P, S], F32, name="yg%d" % t, align_bytes=64) for t in range(PACK)]
-        for t in range(PACK):
+        pair = [held.tile([P, 2 * S], F32, name="pair%d" % t) for t in range(PACK)]
+        den = [held.tile([P, S], F32, name="den%d" % t, align_bytes=64) for t in range(PACK)]
+        inv = [held.tile([P, S], F32, name="inv%d" % t) for t in range(PACK)]
+        z = held.tile([P, PACK, S], F32, name="z")
+        last = PACK - 1
+
+        def denominator(t):
             nc.scalar.activation(wide[t][:, :S], y_acc[t][:], ACT.Square)
-            nc.scalar.activation(sq[t][:], y_acc[t][:], ACT.Square)
-            nc.vector.tensor_tensor(den[t][:], wide[t][:].indirect(l_n1[:]), sq[t][:], ALU.add)
-        for t in range(PACK):
-            nc.scalar.activation(yg[t][:], y_acc[t][:], ACT.Copy, scale=gain[:, t : t + 1])
-            nc.scalar.activation(inv[t][:], den[t][:], ACT.Abs_reciprocal_sqrt, bias=quarter[:])
+            nc.scalar.activation(pair[t][:, S:], y_acc[t][:], ACT.Square)
+            nc.vector.tensor_tensor(den[t][:], wide[t][:].indirect(l_n1[:]), pair[t][:, S:], ALU.add)
 
-        h_acc = [psum.tile([P, S], F32, name="h_acc%d" % t, tag="bank%d" % t) for t in range(PACK)]
+        def normalise(t, chunks):
+            nc.scalar.activation(pair[t][:, :S], y_acc[t][:], ACT.Copy, scale=gain[:, t : t + 1])
+            nc.scalar.activation(inv[t][:], den[t][:], ACT.Abs_reciprocal_sqrt, bias=quarter[:])
+            for lo, hi in chunks:
+                nc.vector.tensor_tensor(z[:, t, lo:hi], pair[t][:].indirect(entries(l_n2, lo, hi)), inv[t][:, lo:hi], ALU.mult)
+
+        denominator(0)
+        for t in range(1, PACK):
+            denominator(t)
+            normalise(t - 1, [(0, S)])
+        w2 = (w2_dealt, deal_scales(nc.vector, w2_plane, "w2_dealt_scales", "den1"))
+        normalise(last, Z_CHUNKS)
+
+        h_acc = [psum.tile([P, S], F32, name="h_acc%d" % b, tag="bank%d" % b) for b in range(PACK)]
+        tail_lo = Z_CHUNKS[-1][0]
+        h_tail = psum.tile([P, S - tail_lo], F32, name="h_tail", tag="bank%d" % (2 * PACK - 1))
+
+        def h_part(t, lo, hi):
+            return h_tail[:] if (t, lo) == (0, tail_lo) else h_acc[t][:, lo:hi]
+
         h = [held.tile([P, S], F32, name="h%d" % t) for t in range(PACK)]
-        z_bf = []
-        for lo, hi in CHUNKS:
-            z = held.tile([P, PACK, hi - lo], F32, name="z%d" % lo)
-            for t in range(PACK):
-                nc.vector.tensor_tensor(z[:, t, :], yg[t][:].indirect(entries(l_n2, lo, hi)), inv[t][:, lo:hi], ALU.mult)
+        for lo, hi in Z_CHUNKS:
             rounded = held.tile([P, PACK * (hi - lo)], BF16, name="z_bf%d" % lo, align_bytes=64)
-            interleave(rounded, z)
-            z_bf.append(rounded)
-        for (lo, hi), rounded in zip(CHUNKS, z_bf):
+            interleave(nc.scalar.copy, rounded, z[:, :, lo:hi])
             z_words = held.tile([P, hi - lo], U32, name="z_words%d" % lo, align_bytes=64)
             z_scales = held.tile([P, hi - lo], U8, name="z_scales%d" % lo, align_bytes=64)
             nc.vector.quantize_mx(out=z_words[:].bitcast(FP8X4), scales=z_scales[:], in_=rounded[:])
             for t in range(PACK):
-                product(h_acc[t][:, lo:hi], w2, t, z_words[:], z_scales[:])
+                product(h_part(t, lo, hi), w2, t, z_words[:], z_scales[:])
 
-        x2_words, x2_scales = pick(l_two, "x2", "yg3", "inv3")
+        def unload(t):
+            for lo, hi in ((0, tail_lo), (tail_lo, S)) if t == 0 else ((0, S),):
+                nc.scalar.copy(wide[t][:, lo:hi], h_part(t, lo, hi))
+                nc.scalar.copy(h[t][:, lo:hi], h_part(t, lo, hi))
+
+        unload(0)
+
+        x2_words = pick_words(l_two, "x2_words", "z_bf%d" % Z_CHUNKS[-1][0])
+        w3 = (deal_words(nc.vector, w3_raw, "w3_dealt", "z_bf0"), deal_scales(nc.vector, w3_plane, "w3_dealt_scales", "z_bf128"))
         d_acc = [psum.tile([P, S], F32, name="d_acc%d" % t, tag="bank%d" % (PACK + t)) for t in range(PACK)]
         for t in range(PACK):
             product(d_acc[t][:], w3, t, x2_words[:], x2_scales[:])
 
-        near = held.tile([P, PACK, S], F32, name="near")
-        far = [held.tile([P, S], F32, name="far%d" % t) for t in range(PACK)]
-        half_d = [held.tile([P, S], F32, name="half_d%d" % t) for t in range(PACK)]
-        for t in range(PACK):
-            nc.scalar.copy(wide[t][:, :S], h_acc[t][:])
-            nc.scalar.copy(h[t][:], h_acc[t][:])
-            diff = held.tile([P, S], F32, name="diff%d" % t)
-            nc.vector.tensor_tensor(diff[:], wide[t][:].indirect(l_n3[:]), h[t][:], ALU.subtract)
-            nc.vector.tensor_tensor(far[t][:], wide[t][:].indirect(l_n4[:]), h[t][:], ALU.subtract)
-            nc.vector.tensor_tensor(near[:, t, :], diff[:], d_acc[t][:], ALU.mult)
-        for t in range(PACK):
-            nc.scalar.activation(half_d[t][:], d_acc[t][:], ACT.Copy, scale=0.5)
-
         out_rows = out_0.rearrange("(p t) j -> p t j", t=PACK)
         out_words = out_1[0].rearrange("p n t -> p (n t)").bitcast(I32)
+        res = held.tile([P, PACK, S], F32, name="res")
         o_scales = held.tile([P, S], U8, name="o_scales", align_bytes=64)
-        o_bf = []
-        for lo, hi in CHUNKS:
-            term = held.tile([P, PACK, hi - lo], F32, name="term%d" % lo)
-            for t in range(PACK):
-                nc.vector.tensor_tensor(term[:, t, :], half_d[t][:].indirect(entries(l_n5, lo, hi)), far[t][:, lo:hi], ALU.mult)
-            res = held.tile([P, PACK, hi - lo], F32, name="res%d" % lo)
-            nc.vector.tensor_tensor(res[:], term[:], near[:, :, lo:hi], ALU.add)
-            nc.sync.dma_start(out_rows[:, :, lo:hi], res[:])
+
+        def weigh(t, lo, hi, far, term):
+            nc.vector.tensor_tensor(term[:, lo:hi], pair[t][:].indirect(entries(l_n5, lo, hi)), far[:, lo:hi], ALU.mult)
+
+        def add_on_tensor(t, near, term):
+            turned = psum.tile([P, PACK, P], F32, name="turned%d" % t, tag="bank%d" % (PACK + t))
+            for b in range(S // P):
+                cols = slice(b * P, (b + 1) * P)
+                nc.tensor.matmul(turned[:, b, :], near[:, cols], ident[:], start=True, stop=False, is_transpose=True)
+                nc.tensor.matmul(turned[:, b, :], term[:, cols], ident[:], start=False, stop=True, is_transpose=True)
+            staged = held.tile([P, PACK, P], F32, name="staged%d" % t)
+            nc.scalar.copy(staged[:], turned[:])
+            back = psum.tile([P, S], F32, name="back%d" % t, tag="bank0")
+            for b in range(S // P):
+                nc.tensor.transpose(back[:, b * P : (b + 1) * P], staged[:, b, :], ident[:])
+            nc.scalar.copy(res[:, t, :], back[:])
+
+        def hand_on(copy, lo, hi):
             rounded = held.tile([P, PACK * (hi - lo)], BF16, name="o_bf%d" % lo, align_bytes=64)
-            interleave(rounded, res)
-            o_bf.append(rounded)
-        for (lo, hi), rounded in zip(CHUNKS, o_bf):
+            interleave(copy, rounded, res[:, :, lo:hi])
             o_words = held.tile([P, hi - lo], U32, name="o_words%d" % lo, align_bytes=64)
             nc.vector.quantize_mx(out=o_words[:].bitcast(FP8X4), scales=o_scales[:, lo:hi], in_=rounded[:])
             nc.sync.dma_start(out_words[:, lo:hi], o_words[:].bitcast(I32))
+
+        for t in range(PACK):
+            nc.scalar.activation(pair[t][:, :S], d_acc[t][:], ACT.Copy, scale=0.5)
+            if t < last:
+                unload(t + 1)
+            diff = held.tile([P, S], F32, name="diff%d" % t)
+            near = held.tile([P, S], F32, name="near%d" % t)
+            far = held.tile([P, S], F32, name="far%d" % t)
+            term = held.tile([P, S], F32, name="term%d" % t)
+            nc.vector.tensor_tensor(diff[:], wide[t][:].indirect(l_n3[:]), h[t][:], ALU.subtract)
+            nc.vector.tensor_tensor(far[:], wide[t][:].indirect(l_n4[:]), h[t][:], ALU.subtract)
+            nc.vector.tensor_tensor(near[:], diff[:], d_acc[t][:], ALU.mult)
+            if t < last:
+                weigh(t, 0, S, far, term)
+                add_on_tensor(t, near, term)
+                nc.sync.dma_start(out_rows[:, t, :], res[:, t, :])
+        for lo, hi in OUT_CHUNKS:
+            weigh(last, lo, hi, far, term)
+            nc.vector.tensor_tensor(res[:, last, lo:hi], near[:, lo:hi], term[:, lo:hi], ALU.add)
+        nc.sync.dma_start(out_rows[:, last, :], res[:, last, :])
+        for lo, hi in OUT_CHUNKS:
+            hand_on(nc.vector.tensor_copy if hi == S else nc.scalar.copy, lo, hi)
         for q in range(4):
             queue = nc.sync if q % 2 else nc.scalar
             queue.dma_start(out_2[0, 4 * q : 4 * q + 4, :].bitcast(I32), o_scales[32 * q : 32 * q + 4, :].bitcast(I32))

@@ -20,7 +20,7 @@ ALU = mybir.AluOpType
 P = 128
 PACK = 4
 LIST_ROWS = 16
-Z_CHUNKS = ((0, 128), (128, 384), (384, 512))
+Z_CHUNKS = ((0, 128), (256, 512), (128, 256))
 OUT_CHUNKS = ((0, 256), (256, 384), (384, 512))
 
 
@@ -121,6 +121,9 @@ def tile_picked_lateflowbrms_none_po_kernel(
         for t in range(PACK):
             nc.scalar.activation(wide[t][:, S:], quarter[:].to_broadcast([P, S]), ACT.Abs_reciprocal_sqrt)
 
+        ident = held.tile([P, P], F32, name="ident")
+        make_identity(nc, ident[:])
+
         w1_dealt = deal_words(nc.vector, w1_raw, "w1_dealt", "w1_dealt")
         xq_scales = pick_scales(l_offs, "xq_scales", "xq_scales")
         xq_words = pick_words(l_offs, "xq_words", "xq_words")
@@ -130,8 +133,7 @@ def tile_picked_lateflowbrms_none_po_kernel(
             product(y_acc[t][:], w1, t, xq_words[:], xq_scales[:])
         x2_scales = pick_scales(l_two, "x2_scales", "x2_scales")
         w2_dealt = deal_words(nc.vector, w2_raw, "w2_dealt", "w2_dealt")
-        ident = held.tile([P, P], F32, name="ident")
-        make_identity(nc, ident[:])
+        w3_dealt = deal_words(nc.gpsimd, w3_raw, "w3_dealt", "w1_plane")
 
         pair = [held.tile([P, 2 * S], F32, name="pair%d" % t) for t in range(PACK)]
         den = [held.tile([P, S], F32, name="den%d" % t, align_bytes=64) for t in range(PACK)]
@@ -158,16 +160,19 @@ def tile_picked_lateflowbrms_none_po_kernel(
         normalise(last, Z_CHUNKS)
 
         h_acc = [psum.tile([P, S], F32, name="h_acc%d" % b, tag="bank%d" % b) for b in range(PACK)]
-        tail_lo = Z_CHUNKS[-1][0]
+        tail_lo = Z_CHUNKS[1][0]
         h_tail = psum.tile([P, S - tail_lo], F32, name="h_tail", tag="bank%d" % (2 * PACK - 1))
 
         def h_part(t, lo, hi):
             return h_tail[:] if (t, lo) == (0, tail_lo) else h_acc[t][:, lo:hi]
 
         h = [held.tile([P, S], F32, name="h%d" % t) for t in range(PACK)]
-        for lo, hi in Z_CHUNKS:
-            rounded = held.tile([P, PACK * (hi - lo)], BF16, name="z_bf%d" % lo, align_bytes=64)
-            interleave(nc.scalar.copy, rounded, z[:, :, lo:hi])
+        z_bf = {}
+        for (lo, hi), copy in zip(Z_CHUNKS, (nc.scalar.copy, nc.scalar.copy, nc.vector.tensor_copy)):
+            z_bf[lo] = held.tile([P, PACK * (hi - lo)], BF16, name="z_bf%d" % lo, align_bytes=64)
+            interleave(copy, z_bf[lo], z[:, :, lo:hi])
+        for lo, hi in sorted(Z_CHUNKS):
+            rounded = z_bf[lo]
             z_words = held.tile([P, hi - lo], U32, name="z_words%d" % lo, align_bytes=64)
             z_scales = held.tile([P, hi - lo], U8, name="z_scales%d" % lo, align_bytes=64)
             nc.vector.quantize_mx(out=z_words[:].bitcast(FP8X4), scales=z_scales[:], in_=rounded[:])
@@ -181,8 +186,8 @@ def tile_picked_lateflowbrms_none_po_kernel(
 
         unload(0)
 
-        x2_words = pick_words(l_two, "x2_words", "z_bf%d" % Z_CHUNKS[-1][0])
-        w3 = (deal_words(nc.vector, w3_raw, "w3_dealt", "z_bf0"), deal_scales(nc.vector, w3_plane, "w3_dealt_scales", "z_bf128"))
+        x2_words = pick_words(l_two, "x2_words", "z_bf%d" % tail_lo)
+        w3 = (w3_dealt, deal_scales(nc.vector, w3_plane, "w3_dealt_scales", "z_bf0"))
         d_acc = [psum.tile([P, S], F32, name="d_acc%d" % t, tag="bank%d" % (PACK + t)) for t in range(PACK)]
         for t in range(PACK):
             product(d_acc[t][:], w3, t, x2_words[:], x2_scales[:])

from contextlib import ExitStack

import concourse.mybir as mybir
from concourse.masks import make_identity

K, T, S, N, H = 512, 2048, 512, 512, 512
FLOPS = 3 * 2 * 512 * 512 * 512

F32 = mybir.dt.float32
BF16 = mybir.dt.bfloat16
I32 = mybir.dt.int32
U32 = mybir.dt.uint32
U16 = mybir.dt.uint16
U8 = mybir.dt.uint8
FP8X4 = mybir.dt.float8_e4m3fn_x4
FP4X4 = mybir.dt.float4_e2m1fn_x4
ACT = mybir.ActivationFunctionType
ALU = mybir.AluOpType

P = 128
PACK = 4
LIST_ROWS = 16
Z_CHUNKS = ((0, 128), (256, 512), (128, 256))
OUT_CHUNKS = ((0, 256), (256, 384), (384, 512))


def tile_picked_lateflowbrms_none_po_kernel(
    tc, x_words, x_scales, w1_words, w1_scales, gn, w2_words, w2_scales, w3_words, w3_scales,
    offs, n1, n2, two, n3, n4, n5, out_0, out_1, out_2,
):
    nc = tc.nc
    with ExitStack() as ctx:
        held = ctx.enter_context(tc.tile_pool(name="held", bufs=1))
        psum = ctx.enter_context(tc.psum_pool(name="psum", bufs=1))

        def load_list(src, name):
            lst = held.tile([P, S // LIST_ROWS], U16, name=name)
            nc.sync.dma_start(lst[:], src)
            return lst

        def load_scale_rows(queues, clear, src, width, name):
            plane = held.tile([P, width], U8, name=name, align_bytes=64)
            clear.memset(plane[:].bitcast(I32), 0)
            for q, queue in enumerate(queues):
                queue.dma_start(plane[32 * q : 32 * q + 4, :].bitcast(I32), src[0, 4 * q : 4 * q + 4, :].bitcast(I32))
            return plane

        def load_weight_words(queue, src, name):
            raw = held.tile([P, 2 * H], U8, name=name, align_bytes=64)
            queue.dma_start(raw[:].bitcast(I32), src[0].bitcast(I32))
            return raw

        def deal_words(engine, raw, name, tag):
            words = held.tile([P, 2 * H], U8, name=name, tag=tag, align_bytes=64)
            engine.tensor_copy(
                words[:].rearrange("p (t m b) -> p t m b", t=PACK, b=2),
                raw[:].rearrange("p (m t b) -> p t m b", t=PACK, b=2),
            )
            return words

        def deal_scales(engine, plane, name, tag):
            scales = held.tile([P, H], U8, name=name, tag=tag, align_bytes=64)
            engine.tensor_copy(
                scales[:].rearrange("p (t m) -> p t m", t=PACK),
                plane[:].rearrange("p (m t) -> p t m", t=PACK),
            )
            return scales

        def pick_words(lst, name, tag):
            words = held.tile([P, S], U32, name=name, tag=tag, align_bytes=64)
            nc.vector.tensor_copy(words[:], xw[:].bitcast(U32).indirect(lst[:]))
            return words

        def pick_scales(lst, name, tag):
            scales = held.tile([P, S], U8, name=name, tag=tag, align_bytes=64)
            nc.vector.tensor_copy(scales[:], xs[:].indirect(lst[:]))
            return scales

        def product(acc, weight, t, words, scales):
            nc.tensor.matmul_mx(
                out=acc,
                lhsT=weight[0][:, 2 * P * t : 2 * P * (t + 1)].bitcast(FP4X4),
                lhsT_scale=weight[1][:, P * t : P * (t + 1)],
                rhs=words.bitcast(FP8X4),
                rhs_scale=scales,
                start=True,
                stop=True,
            )

        def interleave(copy, dst, src):
            copy(
                dst[:].rearrange("p (c i t) -> p c t i", i=4, t=PACK),
                src.rearrange("p t (c i) -> p c t i", i=4),
            )

        def entries(lst, lo, hi):
            return lst[:, lo // LIST_ROWS : hi // LIST_ROWS]

        l_offs = load_list(offs, "l_offs")
        l_two = load_list(two, "l_two")
        xw = held.tile([P, T], I32, name="xw")
        nc.sync.dma_start(xw[:], x_words[0].rearrange("p n t -> p (n t)").bitcast(I32))
        w1_raw = load_weight_words(nc.scalar, w1_words, "w1_raw")
        xs = load_scale_rows([nc.scalar] * 4, nc.gpsimd, x_scales, T, "xs")
        w1_plane = load_scale_rows([nc.sync, nc.sync, nc.sync, nc.gpsimd], nc.gpsimd, w1_scales, H, "w1_plane")
        w2_raw = load_weight_words(nc.sync, w2_words, "w2_raw")
        w3_raw = load_weight_words(nc.sync, w3_words, "w3_raw")
        l_n1 = load_list(n1, "l_n1")
        gain = held.tile([P, PACK], F32, name="gain")
        nc.sync.dma_start(gain[:], gn.rearrange("(p t) o -> p (t o)", t=PACK))
        l_n2 = load_list(n2, "l_n2")
        w2_plane = load_scale_rows([nc.sync] * 4, nc.vector, w2_scales, N, "w2_plane")
        w3_plane = load_scale_rows([nc.sync] * 4, nc.vector, w3_scales, N, "w3_plane")
        l_n3 = load_list(n3, "l_n3")
        l_n4 = load_list(n4, "l_n4")
        l_n5 = load_list(n5, "l_n5")

        quarter = held.tile([P, 1], F32, name="quarter")
        nc.vector.memset(quarter[:], 0.25)
        wide = [held.tile([P, 2 * S], F32, name="wide%d" % t) for t in range(PACK)]
        for t in range(PACK):
            nc.scalar.activation(wide[t][:, S:], quarter[:].to_broadcast([P, S]), ACT.Abs_reciprocal_sqrt)

        ident = held.tile([P, P], F32, name="ident")
        make_identity(nc, ident[:])

        w1_dealt = deal_words(nc.vector, w1_raw, "w1_dealt", "w1_dealt")
        xq_scales = pick_scales(l_offs, "xq_scales", "xq_scales")
        xq_words = pick_words(l_offs, "xq_words", "xq_words")
        w1 = (w1_dealt, deal_scales(nc.vector, w1_plane, "w1_dealt_scales", "w1_dealt_scales"))
        y_acc = [psum.tile([P, S], F32, name="y_acc%d" % t, tag="bank%d" % t) for t in range(PACK)]
        for t in range(PACK):
            product(y_acc[t][:], w1, t, xq_words[:], xq_scales[:])
        x2_scales = pick_scales(l_two, "x2_scales", "x2_scales")
        w2_dealt = deal_words(nc.vector, w2_raw, "w2_dealt", "w2_dealt")
        w3_dealt = deal_words(nc.gpsimd, w3_raw, "w3_dealt", "w1_plane")

        pair = [held.tile([P, 2 * S], F32, name="pair%d" % t) for t in range(PACK)]
        den = [held.tile([P, S], F32, name="den%d" % t, align_bytes=64) for t in range(PACK)]
        inv = [held.tile([P, S], F32, name="inv%d" % t) for t in range(PACK)]
        z = held.tile([P, PACK, S], F32, name="z")
        last = PACK - 1

        def denominator(t):
            nc.scalar.activation(wide[t][:, :S], y_acc[t][:], ACT.Square)
            nc.scalar.activation(pair[t][:, S:], y_acc[t][:], ACT.Square)
            nc.vector.tensor_tensor(den[t][:], wide[t][:].indirect(l_n1[:]), pair[t][:, S:], ALU.add)

        def normalise(t, chunks):
            nc.scalar.activation(pair[t][:, :S], y_acc[t][:], ACT.Copy, scale=gain[:, t : t + 1])
            nc.scalar.activation(inv[t][:], den[t][:], ACT.Abs_reciprocal_sqrt, bias=quarter[:])
            for lo, hi in chunks:
                nc.vector.tensor_tensor(z[:, t, lo:hi], pair[t][:].indirect(entries(l_n2, lo, hi)), inv[t][:, lo:hi], ALU.mult)

        denominator(0)
        for t in range(1, PACK):
            denominator(t)
            normalise(t - 1, [(0, S)])
        w2 = (w2_dealt, deal_scales(nc.vector, w2_plane, "w2_dealt_scales", "den1"))
        normalise(last, Z_CHUNKS)

        h_acc = [psum.tile([P, S], F32, name="h_acc%d" % b, tag="bank%d" % b) for b in range(PACK)]
        tail_lo = Z_CHUNKS[1][0]
        h_tail = psum.tile([P, S - tail_lo], F32, name="h_tail", tag="bank%d" % (2 * PACK - 1))

        def h_part(t, lo, hi):
            return h_tail[:] if (t, lo) == (0, tail_lo) else h_acc[t][:, lo:hi]

        h = [held.tile([P, S], F32, name="h%d" % t) for t in range(PACK)]
        z_bf = {}
        for (lo, hi), copy in zip(Z_CHUNKS, (nc.scalar.copy, nc.scalar.copy, nc.vector.tensor_copy)):
            z_bf[lo] = held.tile([P, PACK * (hi - lo)], BF16, name="z_bf%d" % lo, align_bytes=64)
            interleave(copy, z_bf[lo], z[:, :, lo:hi])
        for lo, hi in sorted(Z_CHUNKS):
            rounded = z_bf[lo]
            z_words = held.tile([P, hi - lo], U32, name="z_words%d" % lo, align_bytes=64)
            z_scales = held.tile([P, hi - lo], U8, name="z_scales%d" % lo, align_bytes=64)
            nc.vector.quantize_mx(out=z_words[:].bitcast(FP8X4), scales=z_scales[:], in_=rounded[:])
            for t in range(PACK):
                product(h_part(t, lo, hi), w2, t, z_words[:], z_scales[:])

        def unload(t):
            for lo, hi in ((0, tail_lo), (tail_lo, S)) if t == 0 else ((0, S),):
                nc.scalar.copy(wide[t][:, lo:hi], h_part(t, lo, hi))
                nc.scalar.copy(h[t][:, lo:hi], h_part(t, lo, hi))

        unload(0)

        x2_words = pick_words(l_two, "x2_words", "z_bf%d" % tail_lo)
        w3 = (w3_dealt, deal_scales(nc.vector, w3_plane, "w3_dealt_scales", "z_bf0"))
        d_acc = [psum.tile([P, S], F32, name="d_acc%d" % t, tag="bank%d" % (PACK + t)) for t in range(PACK)]
        for t in range(PACK):
            product(d_acc[t][:], w3, t, x2_words[:], x2_scales[:])

        out_rows = out_0.rearrange("(p t) j -> p t j", t=PACK)
        out_words = out_1[0].rearrange("p n t -> p (n t)").bitcast(I32)
        res = held.tile([P, PACK, S], F32, name="res")
        o_scales = held.tile([P, S], U8, name="o_scales", align_bytes=64)

        def weigh(t, lo, hi, far, term):
            nc.vector.tensor_tensor(term[:, lo:hi], pair[t][:].indirect(entries(l_n5, lo, hi)), far[:, lo:hi], ALU.mult)

        def add_on_tensor(t, near, term):
            turned = psum.tile([P, PACK, P], F32, name="turned%d" % t, tag="bank%d" % (PACK + t))
            for b in range(S // P):
                cols = slice(b * P, (b + 1) * P)
                nc.tensor.matmul(turned[:, b, :], near[:, cols], ident[:], start=True, stop=False, is_transpose=True)
                nc.tensor.matmul(turned[:, b, :], term[:, cols], ident[:], start=False, stop=True, is_transpose=True)
            staged = held.tile([P, PACK, P], F32, name="staged%d" % t)
            nc.scalar.copy(staged[:], turned[:])
            back = psum.tile([P, S], F32, name="back%d" % t, tag="bank0")
            for b in range(S // P):
                nc.tensor.transpose(back[:, b * P : (b + 1) * P], staged[:, b, :], ident[:])
            nc.scalar.copy(res[:, t, :], back[:])

        def hand_on(copy, lo, hi):
            rounded = held.tile([P, PACK * (hi - lo)], BF16, name="o_bf%d" % lo, align_bytes=64)
            interleave(copy, rounded, res[:, :, lo:hi])
            o_words = held.tile([P, hi - lo], U32, name="o_words%d" % lo, align_bytes=64)
            nc.vector.quantize_mx(out=o_words[:].bitcast(FP8X4), scales=o_scales[:, lo:hi], in_=rounded[:])
            nc.sync.dma_start(out_words[:, lo:hi], o_words[:].bitcast(I32))

        for t in range(PACK):
            nc.scalar.activation(pair[t][:, :S], d_acc[t][:], ACT.Copy, scale=0.5)
            if t < last:
                unload(t + 1)
            diff = held.tile([P, S], F32, name="diff%d" % t)
            near = held.tile([P, S], F32, name="near%d" % t)
            far = held.tile([P, S], F32, name="far%d" % t)
            term = held.tile([P, S], F32, name="term%d" % t)
            nc.vector.tensor_tensor(diff[:], wide[t][:].indirect(l_n3[:]), h[t][:], ALU.subtract)
            nc.vector.tensor_tensor(far[:], wide[t][:].indirect(l_n4[:]), h[t][:], ALU.subtract)
            nc.vector.tensor_tensor(near[:], diff[:], d_acc[t][:], ALU.mult)
            if t < last:
                weigh(t, 0, S, far, term)
                add_on_tensor(t, near, term)
                nc.sync.dma_start(out_rows[:, t, :], res[:, t, :])
        for lo, hi in OUT_CHUNKS:
            weigh(last, lo, hi, far, term)
            nc.vector.tensor_tensor(res[:, last, lo:hi], near[:, lo:hi], term[:, lo:hi], ALU.add)
        nc.sync.dma_start(out_rows[:, last, :], res[:, last, :])
        for lo, hi in OUT_CHUNKS:
            hand_on(nc.vector.tensor_copy if hi == S else nc.scalar.copy, lo, hi)
        for q in range(4):
            queue = nc.sync if q % 2 else nc.scalar
            queue.dma_start(out_2[0, 4 * q : 4 * q + 4, :].bitcast(I32), o_scales[32 * q : 32 * q + 4, :].bitcast(I32))
